import numpy as np
import ml_dtypes


def mxq(x, axis, fmt="e4m3"):
    dtype, down = {"e4m3": (ml_dtypes.float8_e4m3fn, 7), "e5m2": (ml_dtypes.float8_e5m2, 14)}[fmt]
    v = np.moveaxis(np.asarray(x, np.float32).astype(ml_dtypes.bfloat16).astype(np.float64), axis, -1)
    blocks = v.reshape(v.shape[:-1] + (-1, 32))
    amax = np.abs(blocks).max(-1, keepdims=True)
    byte = np.maximum(np.where(amax > 0, np.frexp(amax)[1] - 1 + 127, 0) - down, 1)
    scale = np.exp2(byte - 127.0)
    codes = (blocks / scale).astype(np.float32).astype(dtype).astype(np.float64)
    return np.moveaxis((codes * scale).reshape(v.shape), -1, axis)


WIDE = False


def mx_kscale(k):
    if not WIDE:
        return np.ones(k)
    levels = np.array([10, -10, 5, -5, 0])
    if k % 512:
        return np.exp2(np.random.permutation(np.resize(levels, k // 32))).repeat(32)
    a = np.empty((k // 512, 16))
    for p in range(k // 512):
        a[p, :8] = np.random.permutation(np.resize(levels, 8))
        for g in range(8):
            far = levels[np.abs(levels - a[p, g]) >= 10]
            a[p, g + 8] = far[np.random.randint(len(far))]
    return np.exp2(a.ravel()).repeat(32)


def f64(x):
    return np.asarray(x).astype(np.float64)


def striped(idx):
    return np.tile(np.asarray(idx).reshape(-1, 16).T, (8, 1)).astype(np.uint16)


def unstriped(offs):
    return offs[:16].T.reshape(-1).astype(np.int64)


def striped8(idx):
    return np.asarray(idx).reshape(8, -1, 16).transpose(0, 2, 1).reshape(128, -1).astype(np.uint16)


def unstriped8(offs):
    return offs.reshape(8, 16, -1).transpose(0, 2, 1).reshape(8, -1).astype(np.int64)


def pick8(x, idx, run):
    r = np.arange(len(x))
    return x[r[:, None], idx[r % (8 * run) // run]]


E2M1 = np.array([0.0, 0.5, 1.0, 1.5, 2.0, 3.0, 4.0, 6.0, -0.0, -0.5, -1.0, -1.5, -2.0, -3.0, -4.0, -6.0])


def pack_weight(w, fmt):
    k, n = w.shape
    w = f64(np.asarray(w, np.float32).astype(ml_dtypes.bfloat16)).reshape(k // 32, 32, n)
    amax = np.abs(w).max(1)
    if fmt == "e4m3":
        byte = np.frexp(amax)[1] - 1 + 127 - 7
    else:
        mant, ex = np.frexp(amax / 6.0)
        byte = np.where(mant > 0.5, ex, ex - 1) + 127
    byte = np.clip(np.where(amax > 0, byte, 1), 1, 254)
    scaled = (w * np.exp2(127.0 - byte)[:, None, :]).reshape(k, n).astype(np.float32)
    by_word = np.ascontiguousarray(scaled.reshape(k // 512, 128, 4, n).transpose(0, 1, 3, 2))
    if fmt == "e4m3":
        words = by_word.astype(ml_dtypes.float8_e4m3fn).view(np.uint8)
    else:
        c = by_word.astype(ml_dtypes.float4_e2m1fn).view(np.uint8) & 0xF
        words = (c[..., 0::2] | (c[..., 1::2] << 4)).reshape(k // 512, 128, 2 * n)
    return np.ascontiguousarray(words), np.ascontiguousarray(byte.astype(np.uint8).reshape(k // 512, 16, n))


def unpack_weight(words, scales, fmt):
    g, _, n = scales.shape
    words = np.ascontiguousarray(words).reshape(g, 128, n, -1)
    if fmt == "e4m3":
        vals = words.view(ml_dtypes.float8_e4m3fn).astype(np.float64)
    else:
        nib = np.empty((g, 128, n, 4), np.uint8)
        nib[..., 0::2] = words & 0xF
        nib[..., 1::2] = words >> 4
        vals = E2M1[nib]
    vals = vals * np.repeat(np.exp2(scales.astype(np.float64) - 127.0), 8, axis=1)[..., None]
    return vals.transpose(0, 1, 3, 2).reshape(g * 512, n)


K, J, R, T, U, V, Z, M, O, C, N = 512, 256, 512, 512, 512, 512, 512, 1024, 128, 512, 256


def setup_inputs():
    n = np.random.standard_normal
    idx = np.stack([np.random.permutation(T)[:J] for _ in range(8)])
    idx2 = np.stack([np.random.permutation(U)[:J] for _ in range(8)])
    idx3 = np.stack([np.random.permutation(V)[:J] for _ in range(8)])
    idx4 = np.random.permutation(M)[:J]
    idx5 = np.stack([np.random.permutation(C)[:J] for _ in range(8)])
    idx6 = np.stack([np.random.permutation(C)[:O] for _ in range(8)])
    idx7 = np.stack([np.random.permutation(J)[:O] for _ in range(8)])
    fk = mx_kscale(K)
    fr = mx_kscale(R)
    fz = mx_kscale(Z)
    wp = pack_weight(n((K, R)) * 1 / np.sqrt(K) / fk[:, None] * fr, "e4m3")
    xop = pack_weight(n((Z, M)) / fz[:, None], "e4m3")
    w2p = pack_weight(n((Z, R)) * 1 / np.sqrt(Z) * fz[:, None] * fr, "e2m1")
    wbp = pack_weight(n((R, N)) * 1 / np.sqrt(R) / fr[:, None], "e2m1")
    return {
        "ta": (np.random.randint(-7, 8, (K, T)).astype(np.float64)).astype(np.float32),
        "ga": ((np.random.randint(8, 19, (K, 1)) / 64.0) * fk[:, None]).astype(np.float32),
        "tb": (np.random.randint(-7, 8, (K, U)).astype(np.float64)).astype(np.float32),
        "gb": ((np.random.randint(4, 11, (K, 1)) / 64.0) * fk[:, None]).astype(np.float32),
        "td": (np.random.randint(-7, 8, (K, V)).astype(np.float64)).astype(np.float32),
        "gd": ((np.random.randint(2, 8, (K, 1)) / 64.0) * fk[:, None]).astype(np.float32),
        "w_words": wp[0],
        "w_scales": wp[1],
        "xo_words": xop[0],
        "xo_scales": xop[1],
        "w2_words": w2p[0],
        "w2_scales": w2p[1],
        "sa": (np.random.uniform(0.5, 1.6, (R, 1))).astype(np.float32),
        "sb": (np.random.uniform(0.5, 1.6, (R, 1))).astype(np.float32),
        "wb_words": wbp[0],
        "wb_scales": wbp[1],
        "offs": striped8(idx),
        "offs2": striped8(idx2),
        "offs3": striped8(idx3),
        "offs4": striped(idx4),
        "offs5": striped8(idx5),
        "offs6": striped8(idx6),
        "offs7": striped8(idx7),
    }


def reference(ta, ga, tb, gb, td, gd, w_words, w_scales, xo_words, xo_scales, w2_words, w2_scales, sa, sb, wb_words, wb_scales, offs, offs2, offs3, offs4, offs5, offs6, offs7):
    idx = unstriped8(offs)
    idx2 = unstriped8(offs2)
    idx3 = unstriped8(offs3)
    idx4 = unstriped(offs4)
    idx5 = unstriped8(offs5)
    idx6 = unstriped8(offs6)
    idx7 = unstriped8(offs7)
    wu = unpack_weight(w_words, w_scales, "e4m3")
    xou = unpack_weight(xo_words, xo_scales, "e4m3")
    w2u = unpack_weight(w2_words, w2_scales, "e2m1")
    wbu = unpack_weight(wb_words, wb_scales, "e2m1")
    xc = pick8(f64(ta), idx, 64) * f64(ga) + pick8(f64(tb), idx2, 64) * f64(gb) + pick8(f64(td), idx3, 64) * f64(gd)
    xcq = mxq(xc, 0, "e4m3")
    a = wu.T @ xcq
    xoidx4g = xou[:, idx4]
    b = w2u.T @ xoidx4g
    pw = np.zeros((R, C))
    pw[np.arange(R)[:, None], idx5[np.arange(R) % 512 // 64]] = a
    hid = np.abs(pick8(pw, idx6, 64) * f64(sa) - pick8(b, idx7, 64) * f64(sb))
    hidq = mxq(hid, 0, "e4m3")
    y = wbu.T @ hidq
    return y

@@ -1,0 +1,195 @@
+from contextlib import ExitStack
+
+import concourse.mybir as mybir
+
+F32 = mybir.dt.float32
+BF16 = mybir.dt.bfloat16
+I32 = mybir.dt.int32
+U32 = mybir.dt.uint32
+U16 = mybir.dt.uint16
+U8 = mybir.dt.uint8
+FP8X4 = mybir.dt.float8_e4m3fn_x4
+FP4X4 = mybir.dt.float4_e2m1fn_x4
+ACT = mybir.ActivationFunctionType
+ALU = mybir.AluOpType
+
+P = 128
+PACK = 4
+K, J, R, T, M, O, C, N = 512, 256, 512, 512, 1024, 128, 512, 256
+HALF = J // 2
+FLOPS = 2 * K * R * J + 2 * 512 * R * J + 2 * R * N * O
+
+
+def tile_picked_threebooks_plain_two_boardmeet_one_plain_kernel(
+    tc, ta, ga, tb, gb, td, gd, w_words, w_scales, xo_words, xo_scales, w2_words, w2_scales,
+    sa, sb, wb_words, wb_scales, offs, offs2, offs3, offs4, offs5, offs6, offs7, out,
+):
+    nc = tc.nc
+    with ExitStack() as ctx:
+        pool = ctx.enter_context(tc.tile_pool(name="keep", bufs=1))
+        psum = ctx.enter_context(tc.psum_pool(name="psum", bufs=1))
+
+        def sb_tile(name, shape, dtype):
+            return pool.tile(shape, dtype, name=name, align_bytes=64)
+
+        def load_list(name, src):
+            tile = sb_tile(name, list(src.shape), U16)
+            nc.sync.dma_start(tile[:], src)
+            return tile
+
+        def load_rowvec(name, src, eng):
+            tile = sb_tile(name, [P, PACK], F32)
+            eng.dma_start(tile[:], src.rearrange("(p t) o -> p (t o)", t=PACK))
+            return tile
+
+        def load_table_tile(name, src, t):
+            tile = sb_tile(name, [P, T], F32)
+            nc.sync.dma_start(tile[:], src.rearrange("(p t) c -> p t c", t=PACK)[:, t, :])
+            return tile
+
+        def load_stage(name, src):
+            n = src.shape[2]
+            tile = sb_tile(name, [4, 4, n // 4], I32)
+            nc.gpsimd.dma_start(tile[:], src[0].bitcast(I32).rearrange("(q r) n -> r q n", r=4))
+            return tile
+
+        def spread(plane, stage):
+            for q in range(4):
+                nc.vector.tensor_copy(plane[:].bitcast(I32)[32 * q : 32 * q + 4, :], stage[:, q, :])
+
+        ws_raw = sb_tile("ws_raw", [P, R], U8)
+        w2s_raw = sb_tile("w2s_raw", [P, R], U8)
+        xs_win = sb_tile("xs_win", [P, M], U8)
+        wbs = sb_tile("wbs", [P, N], U8)
+        for plane in (ws_raw, xs_win, w2s_raw, wbs):
+            nc.vector.memset(plane[:].bitcast(I32), 0)
+        board = [sb_tile(f"board{t}", [P, C], F32) for t in range(PACK)]
+        for t in range(PACK):
+            nc.vector.memset(board[t][:], 0.0)
+
+        ga_t = load_rowvec("ga_t", ga, nc.scalar)
+        ta_t = [load_table_tile("ta0", ta, 0)]
+        l1 = load_list("l1", offs)
+        ta_t.extend(load_table_tile(f"ta{t}", ta, t) for t in range(1, PACK))
+        l2 = load_list("l2", offs2)
+        gb_t = load_rowvec("gb_t", gb, nc.sync)
+        tb_t = [load_table_tile(f"tb{t}", tb, t) for t in range(PACK)]
+        l3 = load_list("l3", offs3)
+        gd_t = load_rowvec("gd_t", gd, nc.sync)
+        td_t = [load_table_tile("td0", td, 0)]
+        l4 = load_list("l4", offs4)
+        td_t.append(load_table_tile("td1", td, 1))
+        l5 = load_list("l5", offs5)
+        td_t.extend(load_table_tile(f"td{t}", td, t) for t in range(2, PACK))
+        w_raw = sb_tile("w_raw", [P, R], U32)
+        nc.sync.dma_start(w_raw[:].bitcast(I32), w_words[0].rearrange("p n t -> p (n t)").bitcast(I32))
+        xo_win = sb_tile("xo_win", [P, M], U32)
+        nc.sync.dma_start(xo_win[:].bitcast(I32), xo_words[0].rearrange("p n t -> p (n t)").bitcast(I32))
+        w2_raw = sb_tile("w2_raw", [P, 2 * R], U8)
+        nc.sync.dma_start(w2_raw[:].bitcast(I32), w2_words[0].bitcast(I32))
+        l7 = load_list("l7", offs7)
+        l6 = load_list("l6", offs6)
+        wb_t = sb_tile("wb_t", [P, 2 * N], U8)
+        nc.sync.dma_start(wb_t[:].bitcast(I32), wb_words[0].bitcast(I32))
+
+        ws_st = load_stage("ws_st", w_scales)
+        xs_st = load_stage("xs_st", xo_scales)
+        w2s_st = load_stage("w2s_st", w2_scales)
+        sb_t = load_rowvec("sb_t", sb, nc.gpsimd)
+        sa_t = load_rowvec("sa_t", sa, nc.gpsimd)
+        for q in range(4):
+            nc.gpsimd.dma_start(wbs[:].bitcast(I32)[32 * q : 32 * q + 4, :], wb_scales[0].bitcast(I32)[4 * q : 4 * q + 4, :])
+
+        ws = sb_tile("ws", [P, R], U8)
+        w2s = sb_tile("w2s", [P, R], U8)
+        xs = sb_tile("xs", [P, J], U8)
+        spread(ws_raw, ws_st)
+        spread(xs_win, xs_st)
+        spread(w2s_raw, w2s_st)
+        nc.vector.tensor_copy(ws[:].rearrange("p (t m) -> p t m", t=PACK), ws_raw[:].rearrange("p (m t) -> p t m", t=PACK))
+        nc.vector.tensor_copy(w2s[:].rearrange("p (t m) -> p t m", t=PACK), w2s_raw[:].rearrange("p (m t) -> p t m", t=PACK))
+        nc.vector.tensor_copy(xs[:], xs_win[:].indirect(l4[:]))
+
+        g1 = sb_tile("g1", [P, PACK, J], F32)
+        g2 = sb_tile("g2", [P, PACK, J], F32)
+        g12 = sb_tile("g12", [P, PACK, J], F32)
+        g3 = [sb_tile(f"g3_{h}", [P, PACK, HALF], F32) for h in range(2)]
+        for t in range(PACK):
+            nc.scalar.activation(g1[:, t, :], ta_t[t][:].indirect(l1[:]), ACT.Copy, scale=ga_t[:, t : t + 1])
+        for t in range(PACK):
+            nc.scalar.activation(g2[:, t, :], tb_t[t][:].indirect(l2[:]), ACT.Copy, scale=gb_t[:, t : t + 1])
+            nc.vector.tensor_tensor(g12[:, t, :], g1[:, t, :], g2[:, t, :], ALU.add)
+        hc = HALF // 16
+        for t in range(PACK):
+            for h in range(2):
+                nc.scalar.activation(g3[h][:, t, :], td_t[t][:].indirect(l3[:, h * hc : (h + 1) * hc]), ACT.Copy, scale=gd_t[:, t : t + 1])
+
+        w_d = sb_tile("w_d", [P, PACK, P], U32)
+        for t in range(PACK):
+            nc.scalar.copy(w_d[:, t, :], w_raw[:].rearrange("p (m t) -> p t m", t=PACK)[:, t, :])
+
+        a_sb = []
+        for h in range(2):
+            xc = sb_tile(f"xc{h}", [P, HALF * PACK], BF16)
+            nc.vector.tensor_tensor(
+                xc[:].rearrange("p (c i t) -> p c t i", i=4, t=PACK),
+                g12[:, :, h * HALF : (h + 1) * HALF].rearrange("p t (c i) -> p c t i", i=4),
+                g3[h][:].rearrange("p t (c i) -> p c t i", i=4),
+                ALU.add,
+            )
+            xq = sb_tile(f"xq{h}", [P, HALF], U32)
+            xqs = sb_tile(f"xqs{h}", [P, HALF], U8)
+            nc.vector.quantize_mx(out=xq[:].bitcast(FP8X4), scales=xqs[:], in_=xc[:])
+            a_h = sb_tile(f"a{h}", [P, PACK, HALF], F32)
+            for t in range(PACK):
+                acc = psum.tile([P, HALF], F32, name=f"acc_a{t}", tag=f"bank{t}")
+                nc.tensor.matmul_mx(out=acc[:], lhsT=w_d[:, t, :].bitcast(FP8X4), lhsT_scale=ws[:, t * P : (t + 1) * P],
+                                    rhs=xq[:].bitcast(FP8X4), rhs_scale=xqs[:], start=True, stop=True)
+                nc.scalar.copy(a_h[:, t, :], acc[:])
+            a_sb.append(a_h)
+
+        for t in range(PACK):
+            nc.vector.tensor_copy(board[t][:].indirect(l5[:, 0:hc]), a_sb[0][:, t, :])
+
+        xg = sb_tile("xg", [P, J], U32)
+        nc.vector.tensor_copy(xg[:], xo_win[:].indirect(l4[:]))
+        w2_d = sb_tile("w2_d", [P, 2 * R], U8)
+        nc.scalar.copy(w2_d[:].bitcast(U16).rearrange("p (t m) -> p t m", t=PACK), w2_raw[:].bitcast(U16).rearrange("p (m t) -> p t m", t=PACK))
+        bg = sb_tile("bg", [P, PACK, O], F32)
+        for t in range(PACK):
+            acc = psum.tile([P, J], F32, name=f"acc_b{t}", tag=f"bank{4 + t}")
+            nc.tensor.matmul_mx(out=acc[:], lhsT=w2_d[:, 2 * P * t : 2 * P * (t + 1)].bitcast(FP4X4), lhsT_scale=w2s[:, t * P : (t + 1) * P],
+                                rhs=xg[:].bitcast(FP8X4), rhs_scale=xs[:], start=True, stop=True)
+            b_t = sb_tile(f"b{t}", [P, J], F32)
+            nc.scalar.copy(b_t[:], acc[:])
+            nc.scalar.activation(bg[:, t, :], b_t[:].indirect(l7[:]), ACT.Copy, scale=sb_t[:, t : t + 1])
+
+        ag = sb_tile("ag", [P, PACK, O], F32)
+        diff = sb_tile("diff", [P, PACK, O], F32)
+        for t in range(PACK):
+            nc.vector.tensor_copy(board[t][:].indirect(l5[:, hc : 2 * hc]), a_sb[1][:, t, :])
+            nc.scalar.activation(ag[:, t, :], board[t][:].indirect(l6[:]), ACT.Copy, scale=sa_t[:, t : t + 1])
+        nc.vector.tensor_tensor(diff[:, 0:3, :], ag[:, 0:3, :], bg[:, 0:3, :], ALU.subtract)
+        nc.vector.tensor_tensor(diff[:, 3, :], ag[:, 3, :], bg[:, 3, :], ALU.subtract)
+        hid = sb_tile("hid", [P, O * PACK], BF16)
+        oh = O // 2
+        hv = hid[:].rearrange("p (o t) -> p o t", t=PACK)
+        dv = diff[:].rearrange("p t o -> p o t")
+        nc.scalar.activation(
+            hid[:, 0 : oh * PACK].rearrange("p (c i t) -> p c t i", i=4, t=PACK),
+            diff[:, :, 0:oh].rearrange("p t (c i) -> p c t i", i=4), ACT.Abs)
+        nc.vector.scalar_tensor_tensor(hv[:, oh:O, :], dv[:, oh:O, :], -1.0, dv[:, oh:O, :], ALU.mult, ALU.max)
+        hq = sb_tile("hq", [P, O], U32)
+        hqs = sb_tile("hqs", [P, O], U8)
+        nc.vector.quantize_mx(out=hq[:].bitcast(FP8X4), scales=hqs[:], in_=hid[:])
+        for u in range(N // P):
+            acc = psum.tile([P, O], F32, name=f"acc_y{u}", tag=f"bank{u}")
+            nc.tensor.matmul_mx(out=acc[:], lhsT=wb_t[:, 2 * P * u : 2 * P * (u + 1)].bitcast(FP4X4), lhsT_scale=wbs[:, u * P : (u + 1) * P],
+                                rhs=hq[:].bitcast(FP8X4), rhs_scale=hqs[:], start=True, stop=True)
+            y = sb_tile(f"y{u}", [P, O], F32)
+            if u == 0:
+                nc.vector.tensor_copy(y[:], acc[:])
+                nc.sync.dma_start(out[u * P : (u + 1) * P, :], y[:])
+            else:
+                nc.scalar.copy(y[:], acc[:])
+                nc.scalar.dma_start(out[u * P : (u + 1) * P, :], y[:])

@@ -29,8 +29,8 @@ def tile_picked_threebooks_plain_two_boardmeet_one_plain_kernel(
         pool = ctx.enter_context(tc.tile_pool(name="keep", bufs=1))
         psum = ctx.enter_context(tc.psum_pool(name="psum", bufs=1))
 
-        def sb_tile(name, shape, dtype):
-            return pool.tile(shape, dtype, name=name, align_bytes=64)
+        def sb_tile(name, shape, dtype, tag=None):
+            return pool.tile(shape, dtype, name=name, tag=tag or name, align_bytes=64)
 
         def load_list(name, src):
             tile = sb_tile(name, list(src.shape), U16)
@@ -47,10 +47,10 @@ def tile_picked_threebooks_plain_two_boardmeet_one_plain_kernel(
             nc.sync.dma_start(tile[:], src.rearrange("(p t) c -> p t c", t=PACK)[:, t, :])
             return tile
 
-        def load_stage(name, src):
+        def load_stage(name, src, eng):
             n = src.shape[2]
             tile = sb_tile(name, [4, 4, n // 4], I32)
-            nc.gpsimd.dma_start(tile[:], src[0].bitcast(I32).rearrange("(q r) n -> r q n", r=4))
+            eng.dma_start(tile[:], src[0].bitcast(I32).rearrange("(q r) n -> r q n", r=4))
             return tile
 
         def spread(plane, stage):
@@ -67,38 +67,41 @@ def tile_picked_threebooks_plain_two_boardmeet_one_plain_kernel(
         for t in range(PACK):
             nc.vector.memset(board[t][:], 0.0)
 
+        warm = sb_tile("warm", [P, 2], F32)
+        nc.vector.memset(warm[:, 0:1], 0.0)
+        nc.scalar.activation(warm[:, 1:2], warm[:, 0:1], ACT.Copy)
         ga_t = load_rowvec("ga_t", ga, nc.scalar)
         ta_t = [load_table_tile("ta0", ta, 0)]
         l1 = load_list("l1", offs)
+        ws_st = load_stage("ws_st", w_scales, nc.scalar)
+        xs_st = load_stage("xs_st", xo_scales, nc.scalar)
         ta_t.extend(load_table_tile(f"ta{t}", ta, t) for t in range(1, PACK))
         l2 = load_list("l2", offs2)
-        gb_t = load_rowvec("gb_t", gb, nc.sync)
         tb_t = [load_table_tile(f"tb{t}", tb, t) for t in range(PACK)]
+        w_raw = sb_tile("w_raw", [P, R], U32)
+        nc.sync.dma_start(w_raw[:].bitcast(I32), w_words[0].rearrange("p n t -> p (n t)").bitcast(I32))
         l3 = load_list("l3", offs3)
-        gd_t = load_rowvec("gd_t", gd, nc.sync)
         td_t = [load_table_tile("td0", td, 0)]
         l4 = load_list("l4", offs4)
         td_t.append(load_table_tile("td1", td, 1))
-        l5 = load_list("l5", offs5)
         td_t.extend(load_table_tile(f"td{t}", td, t) for t in range(2, PACK))
-        w_raw = sb_tile("w_raw", [P, R], U32)
-        nc.sync.dma_start(w_raw[:].bitcast(I32), w_words[0].rearrange("p n t -> p (n t)").bitcast(I32))
-        xo_win = sb_tile("xo_win", [P, M], U32)
-        nc.sync.dma_start(xo_win[:].bitcast(I32), xo_words[0].rearrange("p n t -> p (n t)").bitcast(I32))
         w2_raw = sb_tile("w2_raw", [P, 2 * R], U8)
         nc.sync.dma_start(w2_raw[:].bitcast(I32), w2_words[0].bitcast(I32))
+        xo_win = sb_tile("xo_win", [P, M], U32)
+        nc.sync.dma_start(xo_win[:].bitcast(I32), xo_words[0].rearrange("p n t -> p (n t)").bitcast(I32))
+        l5 = load_list("l5", offs5)
         l7 = load_list("l7", offs7)
         l6 = load_list("l6", offs6)
         wb_t = sb_tile("wb_t", [P, 2 * N], U8)
         nc.sync.dma_start(wb_t[:].bitcast(I32), wb_words[0].bitcast(I32))
 
-        ws_st = load_stage("ws_st", w_scales)
-        xs_st = load_stage("xs_st", xo_scales)
-        w2s_st = load_stage("w2s_st", w2_scales)
-        sb_t = load_rowvec("sb_t", sb, nc.gpsimd)
-        sa_t = load_rowvec("sa_t", sa, nc.gpsimd)
+        gb_t = load_rowvec("gb_t", gb, nc.gpsimd)
+        w2s_st = load_stage("w2s_st", w2_scales, nc.gpsimd)
+        gd_t = load_rowvec("gd_t", gd, nc.gpsimd)
+        sb_t = load_rowvec("sb_t", sb, nc.sync)
+        sa_t = load_rowvec("sa_t", sa, nc.sync)
         for q in range(4):
-            nc.gpsimd.dma_start(wbs[:].bitcast(I32)[32 * q : 32 * q + 4, :], wb_scales[0].bitcast(I32)[4 * q : 4 * q + 4, :])
+            nc.sync.dma_start(wbs[:].bitcast(I32)[32 * q : 32 * q + 4, :], wb_scales[0].bitcast(I32)[4 * q : 4 * q + 4, :])
 
         ws = sb_tile("ws", [P, R], U8)
         w2s = sb_tile("w2s", [P, R], U8)
@@ -113,20 +116,22 @@ def tile_picked_threebooks_plain_two_boardmeet_one_plain_kernel(
         g1 = sb_tile("g1", [P, PACK, J], F32)
         g2 = sb_tile("g2", [P, PACK, J], F32)
         g12 = sb_tile("g12", [P, PACK, J], F32)
-        g3 = [sb_tile(f"g3_{h}", [P, PACK, HALF], F32) for h in range(2)]
+        g3 = sb_tile("g3", [P, PACK, J], F32)
         for t in range(PACK):
             nc.scalar.activation(g1[:, t, :], ta_t[t][:].indirect(l1[:]), ACT.Copy, scale=ga_t[:, t : t + 1])
         for t in range(PACK):
             nc.scalar.activation(g2[:, t, :], tb_t[t][:].indirect(l2[:]), ACT.Copy, scale=gb_t[:, t : t + 1])
             nc.vector.tensor_tensor(g12[:, t, :], g1[:, t, :], g2[:, t, :], ALU.add)
         hc = HALF // 16
-        for t in range(PACK):
-            for h in range(2):
-                nc.scalar.activation(g3[h][:, t, :], td_t[t][:].indirect(l3[:, h * hc : (h + 1) * hc]), ACT.Copy, scale=gd_t[:, t : t + 1])
-
         w_d = sb_tile("w_d", [P, PACK, P], U32)
-        for t in range(PACK):
-            nc.scalar.copy(w_d[:, t, :], w_raw[:].rearrange("p (m t) -> p t m", t=PACK)[:, t, :])
+        nc.vector.tensor_copy(w_d[:], w_raw[:].rearrange("p (m t) -> p t m", t=PACK))
+        for t in range(PACK - 1):
+            nc.scalar.activation(g3[:, t, :], td_t[t][:].indirect(l3[:]), ACT.Copy, scale=gd_t[:, t : t + 1])
+        t = PACK - 1
+        for h in range(2):
+            nc.scalar.activation(g3[:, t, h * HALF : (h + 1) * HALF], td_t[t][:].indirect(l3[:, h * hc : (h + 1) * hc]), ACT.Copy, scale=gd_t[:, t : t + 1])
+        w2_d = sb_tile("w2_d", [P, 2 * R], U8)
+        nc.scalar.copy(w2_d[:].bitcast(U16).rearrange("p (t m) -> p t m", t=PACK), w2_raw[:].bitcast(U16).rearrange("p (m t) -> p t m", t=PACK))
 
         a_sb = []
         for h in range(2):
@@ -134,40 +139,40 @@ def tile_picked_threebooks_plain_two_boardmeet_one_plain_kernel(
             nc.vector.tensor_tensor(
                 xc[:].rearrange("p (c i t) -> p c t i", i=4, t=PACK),
                 g12[:, :, h * HALF : (h + 1) * HALF].rearrange("p t (c i) -> p c t i", i=4),
-                g3[h][:].rearrange("p t (c i) -> p c t i", i=4),
+                g3[:, :, h * HALF : (h + 1) * HALF].rearrange("p t (c i) -> p c t i", i=4),
                 ALU.add,
             )
             xq = sb_tile(f"xq{h}", [P, HALF], U32)
             xqs = sb_tile(f"xqs{h}", [P, HALF], U8)
             nc.vector.quantize_mx(out=xq[:].bitcast(FP8X4), scales=xqs[:], in_=xc[:])
-            a_h = sb_tile(f"a{h}", [P, PACK, HALF], F32)
+            a_h = []
             for t in range(PACK):
-                acc = psum.tile([P, HALF], F32, name=f"acc_a{t}", tag=f"bank{t}")
+                acc = psum.tile([P, HALF], F32, name=f"acc_a{t}", tag=f"bank{4 * h + t}")
                 nc.tensor.matmul_mx(out=acc[:], lhsT=w_d[:, t, :].bitcast(FP8X4), lhsT_scale=ws[:, t * P : (t + 1) * P],
                                     rhs=xq[:].bitcast(FP8X4), rhs_scale=xqs[:], start=True, stop=True)
-                nc.scalar.copy(a_h[:, t, :], acc[:])
+                a_t = sb_tile(f"a{h}_{t}", [P, HALF], F32)
+                nc.scalar.copy(a_t[:], acc[:])
+                a_h.append(a_t)
             a_sb.append(a_h)
 
-        for t in range(PACK):
-            nc.vector.tensor_copy(board[t][:].indirect(l5[:, 0:hc]), a_sb[0][:, t, :])
-
-        xg = sb_tile("xg", [P, J], U32)
+        nc.vector.tensor_copy(board[0][:].indirect(l5[:, 0:hc]), a_sb[0][0][:])
+        xg = sb_tile("xg", [P, J], U32, tag="xc0")
         nc.vector.tensor_copy(xg[:], xo_win[:].indirect(l4[:]))
-        w2_d = sb_tile("w2_d", [P, 2 * R], U8)
-        nc.scalar.copy(w2_d[:].bitcast(U16).rearrange("p (t m) -> p t m", t=PACK), w2_raw[:].bitcast(U16).rearrange("p (m t) -> p t m", t=PACK))
+        for t in range(1, PACK):
+            nc.vector.tensor_copy(board[t][:].indirect(l5[:, 0:hc]), a_sb[0][t][:])
         bg = sb_tile("bg", [P, PACK, O], F32)
         for t in range(PACK):
-            acc = psum.tile([P, J], F32, name=f"acc_b{t}", tag=f"bank{4 + t}")
+            acc = psum.tile([P, J], F32, name=f"acc_b{t}", tag=f"bank{t}")
             nc.tensor.matmul_mx(out=acc[:], lhsT=w2_d[:, 2 * P * t : 2 * P * (t + 1)].bitcast(FP4X4), lhsT_scale=w2s[:, t * P : (t + 1) * P],
                                 rhs=xg[:].bitcast(FP8X4), rhs_scale=xs[:], start=True, stop=True)
             b_t = sb_tile(f"b{t}", [P, J], F32)
             nc.scalar.copy(b_t[:], acc[:])
             nc.scalar.activation(bg[:, t, :], b_t[:].indirect(l7[:]), ACT.Copy, scale=sb_t[:, t : t + 1])
 
-        ag = sb_tile("ag", [P, PACK, O], F32)
+        ag = sb_tile("ag", [P, PACK, O], F32, tag="b3")
         diff = sb_tile("diff", [P, PACK, O], F32)
         for t in range(PACK):
-            nc.vector.tensor_copy(board[t][:].indirect(l5[:, hc : 2 * hc]), a_sb[1][:, t, :])
+            nc.vector.tensor_copy(board[t][:].indirect(l5[:, hc : 2 * hc]), a_sb[1][t][:])
             nc.scalar.activation(ag[:, t, :], board[t][:].indirect(l6[:]), ACT.Copy, scale=sa_t[:, t : t + 1])
         nc.vector.tensor_tensor(diff[:, 0:3, :], ag[:, 0:3, :], bg[:, 0:3, :], ALU.subtract)
         nc.vector.tensor_tensor(diff[:, 3, :], ag[:, 3, :], bg[:, 3, :], ALU.subtract)
@@ -183,7 +188,7 @@ def tile_picked_threebooks_plain_two_boardmeet_one_plain_kernel(
         hqs = sb_tile("hqs", [P, O], U8)
         nc.vector.quantize_mx(out=hq[:].bitcast(FP8X4), scales=hqs[:], in_=hid[:])
         for u in range(N // P):
-            acc = psum.tile([P, O], F32, name=f"acc_y{u}", tag=f"bank{u}")
+            acc = psum.tile([P, O], F32, name=f"acc_y{u}", tag=f"bank{4 + u}")
             nc.tensor.matmul_mx(out=acc[:], lhsT=wb_t[:, 2 * P * u : 2 * P * (u + 1)].bitcast(FP4X4), lhsT_scale=wbs[:, u * P : (u + 1) * P],
                                 rhs=hq[:].bitcast(FP8X4), rhs_scale=hqs[:], start=True, stop=True)
             y = sb_tile(f"y{u}", [P, O], F32)

@@ -73,33 +73,34 @@ def tile_picked_threebooks_plain_two_boardmeet_one_plain_kernel(
         ga_t = load_rowvec("ga_t", ga, nc.scalar)
         ta_t = [load_table_tile("ta0", ta, 0)]
         l1 = load_list("l1", offs)
-        ws_st = load_stage("ws_st", w_scales, nc.scalar)
-        xs_st = load_stage("xs_st", xo_scales, nc.scalar)
-        ta_t.extend(load_table_tile(f"ta{t}", ta, t) for t in range(1, PACK))
+        ta_t.append(load_table_tile("ta1", ta, 1))
+        ws_st = load_stage("ws_st", w_scales, nc.sync)
+        ta_t.append(load_table_tile("ta2", ta, 2))
+        xs_st = load_stage("xs_st", xo_scales, nc.sync)
+        ta_t.append(load_table_tile("ta3", ta, 3))
         l2 = load_list("l2", offs2)
-        tb_t = [load_table_tile(f"tb{t}", tb, t) for t in range(PACK)]
+        gb_t = load_rowvec("gb_t", gb, nc.sync)
+        tb_t = [load_table_tile(f"tb{t}", tb, t) for t in range(2)]
+        w2s_st = load_stage("w2s_st", w2_scales, nc.sync)
+        l4 = load_list("l4", offs4)
+        tb_t.extend(load_table_tile(f"tb{t}", tb, t) for t in range(2, PACK))
+        l3 = load_list("l3", offs3)
+        gd_t = load_rowvec("gd_t", gd, nc.sync)
+        td_t = [load_table_tile(f"td{t}", td, t) for t in range(PACK)]
         w_raw = sb_tile("w_raw", [P, R], U32)
         nc.sync.dma_start(w_raw[:].bitcast(I32), w_words[0].rearrange("p n t -> p (n t)").bitcast(I32))
-        l3 = load_list("l3", offs3)
-        td_t = [load_table_tile("td0", td, 0)]
-        l4 = load_list("l4", offs4)
-        td_t.append(load_table_tile("td1", td, 1))
-        td_t.extend(load_table_tile(f"td{t}", td, t) for t in range(2, PACK))
-        w2_raw = sb_tile("w2_raw", [P, 2 * R], U8)
-        nc.sync.dma_start(w2_raw[:].bitcast(I32), w2_words[0].bitcast(I32))
+        l5 = load_list("l5", offs5)
         xo_win = sb_tile("xo_win", [P, M], U32)
         nc.sync.dma_start(xo_win[:].bitcast(I32), xo_words[0].rearrange("p n t -> p (n t)").bitcast(I32))
-        l5 = load_list("l5", offs5)
+        w2_raw = sb_tile("w2_raw", [P, 2 * R], U8)
+        nc.sync.dma_start(w2_raw[:].bitcast(I32), w2_words[0].bitcast(I32))
         l7 = load_list("l7", offs7)
+        sb_t = load_rowvec("sb_t", sb, nc.sync)
         l6 = load_list("l6", offs6)
+        sa_t = load_rowvec("sa_t", sa, nc.sync)
         wb_t = sb_tile("wb_t", [P, 2 * N], U8)
         nc.sync.dma_start(wb_t[:].bitcast(I32), wb_words[0].bitcast(I32))
 
-        gb_t = load_rowvec("gb_t", gb, nc.gpsimd)
-        w2s_st = load_stage("w2s_st", w2_scales, nc.gpsimd)
-        gd_t = load_rowvec("gd_t", gd, nc.gpsimd)
-        sb_t = load_rowvec("sb_t", sb, nc.sync)
-        sa_t = load_rowvec("sa_t", sa, nc.sync)
         for q in range(4):
             nc.sync.dma_start(wbs[:].bitcast(I32)[32 * q : 32 * q + 4, :], wb_scales[0].bitcast(I32)[4 * q : 4 * q + 4, :])
 
@@ -123,43 +124,47 @@ def tile_picked_threebooks_plain_two_boardmeet_one_plain_kernel(
             nc.scalar.activation(g2[:, t, :], tb_t[t][:].indirect(l2[:]), ACT.Copy, scale=gb_t[:, t : t + 1])
             nc.vector.tensor_tensor(g12[:, t, :], g1[:, t, :], g2[:, t, :], ALU.add)
         hc = HALF // 16
-        w_d = sb_tile("w_d", [P, PACK, P], U32)
-        nc.vector.tensor_copy(w_d[:], w_raw[:].rearrange("p (m t) -> p t m", t=PACK))
+        xsum = sb_tile("xsum", [P, PACK, J], F32)
         for t in range(PACK - 1):
             nc.scalar.activation(g3[:, t, :], td_t[t][:].indirect(l3[:]), ACT.Copy, scale=gd_t[:, t : t + 1])
+            nc.vector.tensor_tensor(xsum[:, t, :], g12[:, t, :], g3[:, t, :], ALU.add)
         t = PACK - 1
         for h in range(2):
-            nc.scalar.activation(g3[:, t, h * HALF : (h + 1) * HALF], td_t[t][:].indirect(l3[:, h * hc : (h + 1) * hc]), ACT.Copy, scale=gd_t[:, t : t + 1])
-        w2_d = sb_tile("w2_d", [P, 2 * R], U8)
-        nc.scalar.copy(w2_d[:].bitcast(U16).rearrange("p (t m) -> p t m", t=PACK), w2_raw[:].bitcast(U16).rearrange("p (m t) -> p t m", t=PACK))
+            cols = slice(h * HALF, (h + 1) * HALF)
+            nc.scalar.activation(g3[:, t, cols], td_t[t][:].indirect(l3[:, h * hc : (h + 1) * hc]), ACT.Copy, scale=gd_t[:, t : t + 1])
+            nc.vector.tensor_tensor(xsum[:, t, cols], g12[:, t, cols], g3[:, t, cols], ALU.add)
+        w_d = sb_tile("w_d", [P, PACK, P], U32)
+        for t in range(PACK):
+            nc.scalar.copy(w_d[:, t, :], w_raw[:].rearrange("p (m t) -> p t m", t=PACK)[:, t, :])
 
+        xc = []
+        for h in range(2):
+            xc_h = sb_tile(f"xc{h}", [P, HALF, PACK], BF16)
+            nc.vector.tensor_copy(xc_h[:], xsum[:, :, h * HALF : (h + 1) * HALF].rearrange("p t j -> p j t"))
+            xc.append(xc_h)
         a_sb = []
         for h in range(2):
-            xc = sb_tile(f"xc{h}", [P, HALF * PACK], BF16)
-            nc.vector.tensor_tensor(
-                xc[:].rearrange("p (c i t) -> p c t i", i=4, t=PACK),
-                g12[:, :, h * HALF : (h + 1) * HALF].rearrange("p t (c i) -> p c t i", i=4),
-                g3[:, :, h * HALF : (h + 1) * HALF].rearrange("p t (c i) -> p c t i", i=4),
-                ALU.add,
-            )
             xq = sb_tile(f"xq{h}", [P, HALF], U32)
             xqs = sb_tile(f"xqs{h}", [P, HALF], U8)
-            nc.vector.quantize_mx(out=xq[:].bitcast(FP8X4), scales=xqs[:], in_=xc[:])
+            nc.vector.quantize_mx(out=xq[:].bitcast(FP8X4), scales=xqs[:], in_=xc[h][:].rearrange("p j t -> p (j t)"))
             a_h = []
-            for t in range(PACK):
-                acc = psum.tile([P, HALF], F32, name=f"acc_a{t}", tag=f"bank{4 * h + t}")
-                nc.tensor.matmul_mx(out=acc[:], lhsT=w_d[:, t, :].bitcast(FP8X4), lhsT_scale=ws[:, t * P : (t + 1) * P],
-                                    rhs=xq[:].bitcast(FP8X4), rhs_scale=xqs[:], start=True, stop=True)
-                a_t = sb_tile(f"a{h}_{t}", [P, HALF], F32)
-                nc.scalar.copy(a_t[:], acc[:])
-                a_h.append(a_t)
+            for g, ts in enumerate(((0,), (1, 2, 3)) if h == 0 else ((0, 1, 2, 3),)):
+                acc = psum.tile([P, len(ts), HALF], F32, name=f"acc_a{h}{g}", tag=f"bank{4 + 2 * h + g}")
+                for i, t in enumerate(ts):
+                    nc.tensor.matmul_mx(out=acc[:, i, :], lhsT=w_d[:, t, :].bitcast(FP8X4), lhsT_scale=ws[:, t * P : (t + 1) * P],
+                                        rhs=xq[:].bitcast(FP8X4), rhs_scale=xqs[:], start=True, stop=True)
+                a_g = sb_tile(f"a{h}_{g}", [P, len(ts), HALF], F32)
+                nc.scalar.copy(a_g[:], acc[:])
+                a_h.extend(a_g[:, i, :] for i in range(len(ts)))
             a_sb.append(a_h)
 
-        nc.vector.tensor_copy(board[0][:].indirect(l5[:, 0:hc]), a_sb[0][0][:])
-        xg = sb_tile("xg", [P, J], U32, tag="xc0")
+        nc.vector.tensor_copy(board[0][:].indirect(l5[:, 0:hc]), a_sb[0][0])
+        xg = sb_tile("xg", [P, J], U32, tag="xc1")
         nc.vector.tensor_copy(xg[:], xo_win[:].indirect(l4[:]))
         for t in range(1, PACK):
-            nc.vector.tensor_copy(board[t][:].indirect(l5[:, 0:hc]), a_sb[0][t][:])
+            nc.vector.tensor_copy(board[t][:].indirect(l5[:, 0:hc]), a_sb[0][t])
+        w2_d = sb_tile("w2_d", [P, 2 * R], U8, tag="w_d")
+        nc.scalar.copy(w2_d[:].bitcast(U16).rearrange("p (t m) -> p t m", t=PACK), w2_raw[:].bitcast(U16).rearrange("p (m t) -> p t m", t=PACK))
         bg = sb_tile("bg", [P, PACK, O], F32)
         for t in range(PACK):
             acc = psum.tile([P, J], F32, name=f"acc_b{t}", tag=f"bank{t}")
@@ -172,7 +177,7 @@ def tile_picked_threebooks_plain_two_boardmeet_one_plain_kernel(
         ag = sb_tile("ag", [P, PACK, O], F32, tag="b3")
         diff = sb_tile("diff", [P, PACK, O], F32)
         for t in range(PACK):
-            nc.vector.tensor_copy(board[t][:].indirect(l5[:, hc : 2 * hc]), a_sb[1][t][:])
+            nc.vector.tensor_copy(board[t][:].indirect(l5[:, hc : 2 * hc]), a_sb[1][t])
             nc.scalar.activation(ag[:, t, :], board[t][:].indirect(l6[:]), ACT.Copy, scale=sa_t[:, t : t + 1])
         nc.vector.tensor_tensor(diff[:, 0:3, :], ag[:, 0:3, :], bg[:, 0:3, :], ALU.subtract)
         nc.vector.tensor_tensor(diff[:, 3, :], ag[:, 3, :], bg[:, 3, :], ALU.subtract)
@@ -180,9 +185,7 @@ def tile_picked_threebooks_plain_two_boardmeet_one_plain_kernel(
         oh = O // 2
         hv = hid[:].rearrange("p (o t) -> p o t", t=PACK)
         dv = diff[:].rearrange("p t o -> p o t")
-        nc.scalar.activation(
-            hid[:, 0 : oh * PACK].rearrange("p (c i t) -> p c t i", i=4, t=PACK),
-            diff[:, :, 0:oh].rearrange("p t (c i) -> p c t i", i=4), ACT.Abs)
+        nc.scalar.activation(hv[:, 0:oh, :], dv[:, 0:oh, :], ACT.Abs)
         nc.vector.scalar_tensor_tensor(hv[:, oh:O, :], dv[:, oh:O, :], -1.0, dv[:, oh:O, :], ALU.mult, ALU.max)
         hq = sb_tile("hq", [P, O], U32)
         hqs = sb_tile("hqs", [P, O], U8)

from contextlib import ExitStack

import concourse.mybir as mybir

F32 = mybir.dt.float32
BF16 = mybir.dt.bfloat16
I32 = mybir.dt.int32
U32 = mybir.dt.uint32
U16 = mybir.dt.uint16
U8 = mybir.dt.uint8
FP8X4 = mybir.dt.float8_e4m3fn_x4
FP4X4 = mybir.dt.float4_e2m1fn_x4
ACT = mybir.ActivationFunctionType
ALU = mybir.AluOpType

P = 128
PACK = 4
K, J, R, T, M, O, C, N = 512, 256, 512, 512, 1024, 128, 512, 256
HALF = J // 2
FLOPS = 2 * K * R * J + 2 * 512 * R * J + 2 * R * N * O


def tile_picked_threebooks_plain_two_boardmeet_one_plain_kernel(
    tc, ta, ga, tb, gb, td, gd, w_words, w_scales, xo_words, xo_scales, w2_words, w2_scales,
    sa, sb, wb_words, wb_scales, offs, offs2, offs3, offs4, offs5, offs6, offs7, out,
):
    nc = tc.nc
    with ExitStack() as ctx:
        pool = ctx.enter_context(tc.tile_pool(name="keep", bufs=1))
        psum = ctx.enter_context(tc.psum_pool(name="psum", bufs=1))

        def sb_tile(name, shape, dtype, tag=None):
            return pool.tile(shape, dtype, name=name, tag=tag or name, align_bytes=64)

        def load_list(name, src):
            tile = sb_tile(name, list(src.shape), U16)
            nc.sync.dma_start(tile[:], src)
            return tile

        def load_rowvec(name, src, eng):
            tile = sb_tile(name, [P, PACK], F32)
            eng.dma_start(tile[:], src.rearrange("(p t) o -> p (t o)", t=PACK))
            return tile

        def load_table_tile(name, src, t):
            tile = sb_tile(name, [P, T], F32)
            nc.sync.dma_start(tile[:], src.rearrange("(p t) c -> p t c", t=PACK)[:, t, :])
            return tile

        def load_stage(name, src, eng):
            n = src.shape[2]
            tile = sb_tile(name, [4, 4, n // 4], I32)
            eng.dma_start(tile[:], src[0].bitcast(I32).rearrange("(q r) n -> r q n", r=4))
            return tile

        def spread(plane, stage):
            for q in range(4):
                nc.vector.tensor_copy(plane[:].bitcast(I32)[32 * q : 32 * q + 4, :], stage[:, q, :])

        ws_raw = sb_tile("ws_raw", [P, R], U8)
        w2s_raw = sb_tile("w2s_raw", [P, R], U8)
        xs_win = sb_tile("xs_win", [P, M], U8)
        wbs = sb_tile("wbs", [P, N], U8)
        for plane in (ws_raw, xs_win, w2s_raw, wbs):
            nc.vector.memset(plane[:].bitcast(I32), 0)
        board = [sb_tile(f"board{t}", [P, C], F32) for t in range(PACK)]
        for t in range(PACK):
            nc.vector.memset(board[t][:], 0.0)

        warm = sb_tile("warm", [P, 2], F32)
        nc.vector.memset(warm[:, 0:1], 0.0)
        nc.scalar.activation(warm[:, 1:2], warm[:, 0:1], ACT.Copy)
        ga_t = load_rowvec("ga_t", ga, nc.scalar)
        ta_t = [load_table_tile("ta0", ta, 0)]
        l1 = load_list("l1", offs)
        ta_t.append(load_table_tile("ta1", ta, 1))
        ws_st = load_stage("ws_st", w_scales, nc.sync)
        ta_t.append(load_table_tile("ta2", ta, 2))
        xs_st = load_stage("xs_st", xo_scales, nc.sync)
        ta_t.append(load_table_tile("ta3", ta, 3))
        l2 = load_list("l2", offs2)
        gb_t = load_rowvec("gb_t", gb, nc.sync)
        tb_t = [load_table_tile(f"tb{t}", tb, t) for t in range(2)]
        w2s_st = load_stage("w2s_st", w2_scales, nc.sync)
        l4 = load_list("l4", offs4)
        tb_t.extend(load_table_tile(f"tb{t}", tb, t) for t in range(2, PACK))
        l3 = load_list("l3", offs3)
        gd_t = load_rowvec("gd_t", gd, nc.sync)
        td_t = [load_table_tile(f"td{t}", td, t) for t in range(PACK)]
        w_raw = sb_tile("w_raw", [P, R], U32)
        nc.sync.dma_start(w_raw[:].bitcast(I32), w_words[0].rearrange("p n t -> p (n t)").bitcast(I32))
        l5 = load_list("l5", offs5)
        xo_win = sb_tile("xo_win", [P, M], U32)
        nc.sync.dma_start(xo_win[:].bitcast(I32), xo_words[0].rearrange("p n t -> p (n t)").bitcast(I32))
        w2_raw = sb_tile("w2_raw", [P, 2 * R], U8)
        nc.sync.dma_start(w2_raw[:].bitcast(I32), w2_words[0].bitcast(I32))
        l7 = load_list("l7", offs7)
        sb_t = load_rowvec("sb_t", sb, nc.sync)
        l6 = load_list("l6", offs6)
        sa_t = load_rowvec("sa_t", sa, nc.sync)
        wb_t = sb_tile("wb_t", [P, 2 * N], U8)
        nc.sync.dma_start(wb_t[:].bitcast(I32), wb_words[0].bitcast(I32))

        for q in range(4):
            nc.sync.dma_start(wbs[:].bitcast(I32)[32 * q : 32 * q + 4, :], wb_scales[0].bitcast(I32)[4 * q : 4 * q + 4, :])

        ws = sb_tile("ws", [P, R], U8)
        w2s = sb_tile("w2s", [P, R], U8)
        xs = sb_tile("xs", [P, J], U8)
        spread(ws_raw, ws_st)
        spread(xs_win, xs_st)
        spread(w2s_raw, w2s_st)
        nc.vector.tensor_copy(ws[:].rearrange("p (t m) -> p t m", t=PACK), ws_raw[:].rearrange("p (m t) -> p t m", t=PACK))
        nc.vector.tensor_copy(w2s[:].rearrange("p (t m) -> p t m", t=PACK), w2s_raw[:].rearrange("p (m t) -> p t m", t=PACK))
        nc.vector.tensor_copy(xs[:], xs_win[:].indirect(l4[:]))

        g1 = sb_tile("g1", [P, PACK, J], F32)
        g2 = sb_tile("g2", [P, PACK, J], F32)
        g12 = sb_tile("g12", [P, PACK, J], F32)
        g3 = sb_tile("g3", [P, PACK, J], F32)
        for t in range(PACK):
            nc.scalar.activation(g1[:, t, :], ta_t[t][:].indirect(l1[:]), ACT.Copy, scale=ga_t[:, t : t + 1])
        for t in range(PACK):
            nc.scalar.activation(g2[:, t, :], tb_t[t][:].indirect(l2[:]), ACT.Copy, scale=gb_t[:, t : t + 1])
            nc.vector.tensor_tensor(g12[:, t, :], g1[:, t, :], g2[:, t, :], ALU.add)
        hc = HALF // 16
        xsum = sb_tile("xsum", [P, PACK, J], F32)
        for t in range(PACK - 1):
            nc.scalar.activation(g3[:, t, :], td_t[t][:].indirect(l3[:]), ACT.Copy, scale=gd_t[:, t : t + 1])
            nc.vector.tensor_tensor(xsum[:, t, :], g12[:, t, :], g3[:, t, :], ALU.add)
        t = PACK - 1
        for h in range(2):
            cols = slice(h * HALF, (h + 1) * HALF)
            nc.scalar.activation(g3[:, t, cols], td_t[t][:].indirect(l3[:, h * hc : (h + 1) * hc]), ACT.Copy, scale=gd_t[:, t : t + 1])
            nc.vector.tensor_tensor(xsum[:, t, cols], g12[:, t, cols], g3[:, t, cols], ALU.add)
        w_d = sb_tile("w_d", [P, PACK, P], U32)
        for t in range(PACK):
            nc.scalar.copy(w_d[:, t, :], w_raw[:].rearrange("p (m t) -> p t m", t=PACK)[:, t, :])

        xc = []
        for h in range(2):
            xc_h = sb_tile(f"xc{h}", [P, HALF, PACK], BF16)
            nc.vector.tensor_copy(xc_h[:], xsum[:, :, h * HALF : (h + 1) * HALF].rearrange("p t j -> p j t"))
            xc.append(xc_h)
        a_sb = []
        for h in range(2):
            xq = sb_tile(f"xq{h}", [P, HALF], U32)
            xqs = sb_tile(f"xqs{h}", [P, HALF], U8)
            nc.vector.quantize_mx(out=xq[:].bitcast(FP8X4), scales=xqs[:], in_=xc[h][:].rearrange("p j t -> p (j t)"))
            a_h = []
            for g, ts in enumerate(((0,), (1, 2, 3)) if h == 0 else ((0, 1, 2, 3),)):
                acc = psum.tile([P, len(ts), HALF], F32, name=f"acc_a{h}{g}", tag=f"bank{4 + 2 * h + g}")
                for i, t in enumerate(ts):
                    nc.tensor.matmul_mx(out=acc[:, i, :], lhsT=w_d[:, t, :].bitcast(FP8X4), lhsT_scale=ws[:, t * P : (t + 1) * P],
                                        rhs=xq[:].bitcast(FP8X4), rhs_scale=xqs[:], start=True, stop=True)
                a_g = sb_tile(f"a{h}_{g}", [P, len(ts), HALF], F32)
                nc.scalar.copy(a_g[:], acc[:])
                a_h.extend(a_g[:, i, :] for i in range(len(ts)))
            a_sb.append(a_h)

        nc.vector.tensor_copy(board[0][:].indirect(l5[:, 0:hc]), a_sb[0][0])
        xg = sb_tile("xg", [P, J], U32, tag="xc1")
        nc.vector.tensor_copy(xg[:], xo_win[:].indirect(l4[:]))
        for t in range(1, PACK):
            nc.vector.tensor_copy(board[t][:].indirect(l5[:, 0:hc]), a_sb[0][t])
        w2_d = sb_tile("w2_d", [P, 2 * R], U8, tag="w_d")
        nc.scalar.copy(w2_d[:].bitcast(U16).rearrange("p (t m) -> p t m", t=PACK), w2_raw[:].bitcast(U16).rearrange("p (m t) -> p t m", t=PACK))
        bg = sb_tile("bg", [P, PACK, O], F32)
        for t in range(PACK):
            acc = psum.tile([P, J], F32, name=f"acc_b{t}", tag=f"bank{t}")
            nc.tensor.matmul_mx(out=acc[:], lhsT=w2_d[:, 2 * P * t : 2 * P * (t + 1)].bitcast(FP4X4), lhsT_scale=w2s[:, t * P : (t + 1) * P],
                                rhs=xg[:].bitcast(FP8X4), rhs_scale=xs[:], start=True, stop=True)
            b_t = sb_tile(f"b{t}", [P, J], F32)
            nc.scalar.copy(b_t[:], acc[:])
            nc.scalar.activation(bg[:, t, :], b_t[:].indirect(l7[:]), ACT.Copy, scale=sb_t[:, t : t + 1])

        ag = sb_tile("ag", [P, PACK, O], F32, tag="b3")
        diff = sb_tile("diff", [P, PACK, O], F32)
        for t in range(PACK):
            nc.vector.tensor_copy(board[t][:].indirect(l5[:, hc : 2 * hc]), a_sb[1][t])
            nc.scalar.activation(ag[:, t, :], board[t][:].indirect(l6[:]), ACT.Copy, scale=sa_t[:, t : t + 1])
        nc.vector.tensor_tensor(diff[:, 0:3, :], ag[:, 0:3, :], bg[:, 0:3, :], ALU.subtract)
        nc.vector.tensor_tensor(diff[:, 3, :], ag[:, 3, :], bg[:, 3, :], ALU.subtract)
        hid = sb_tile("hid", [P, O * PACK], BF16)
        oh = O // 2
        hv = hid[:].rearrange("p (o t) -> p o t", t=PACK)
        dv = diff[:].rearrange("p t o -> p o t")
        nc.scalar.activation(hv[:, 0:oh, :], dv[:, 0:oh, :], ACT.Abs)
        nc.vector.scalar_tensor_tensor(hv[:, oh:O, :], dv[:, oh:O, :], -1.0, dv[:, oh:O, :], ALU.mult, ALU.max)
        hq = sb_tile("hq", [P, O], U32)
        hqs = sb_tile("hqs", [P, O], U8)
        nc.vector.quantize_mx(out=hq[:].bitcast(FP8X4), scales=hqs[:], in_=hid[:])
        for u in range(N // P):
            acc = psum.tile([P, O], F32, name=f"acc_y{u}", tag=f"bank{4 + u}")
            nc.tensor.matmul_mx(out=acc[:], lhsT=wb_t[:, 2 * P * u : 2 * P * (u + 1)].bitcast(FP4X4), lhsT_scale=wbs[:, u * P : (u + 1) * P],
                                rhs=hq[:].bitcast(FP8X4), rhs_scale=hqs[:], start=True, stop=True)
            y = sb_tile(f"y{u}", [P, O], F32)
            if u == 0:
                nc.vector.tensor_copy(y[:], acc[:])
                nc.sync.dma_start(out[u * P : (u + 1) * P, :], y[:])
            else:
                nc.scalar.copy(y[:], acc[:])
                nc.scalar.dma_start(out[u * P : (u + 1) * P, :], y[:])
